import numpy as np
import ml_dtypes


def mxq(x, axis, fmt="e4m3"):
    dtype, down = {"e4m3": (ml_dtypes.float8_e4m3fn, 7), "e5m2": (ml_dtypes.float8_e5m2, 14)}[fmt]
    v = np.moveaxis(np.asarray(x, np.float32).astype(ml_dtypes.bfloat16).astype(np.float64), axis, -1)
    blocks = v.reshape(v.shape[:-1] + (-1, 32))
    amax = np.abs(blocks).max(-1, keepdims=True)
    byte = np.maximum(np.where(amax > 0, np.frexp(amax)[1] - 1 + 127, 0) - down, 1)
    scale = np.exp2(byte - 127.0)
    codes = (blocks / scale).astype(np.float32).astype(dtype).astype(np.float64)
    return np.moveaxis((codes * scale).reshape(v.shape), -1, axis)


WIDE = False


def mx_kscale(k):
    if not WIDE:
        return np.ones(k)
    levels = np.array([10, -10, 5, -5, 0])
    if k % 512:
        return np.exp2(np.random.permutation(np.resize(levels, k // 32))).repeat(32)
    a = np.empty((k // 512, 16))
    for p in range(k // 512):
        a[p, :8] = np.random.permutation(np.resize(levels, 8))
        for g in range(8):
            far = levels[np.abs(levels - a[p, g]) >= 10]
            a[p, g + 8] = far[np.random.randint(len(far))]
    return np.exp2(a.ravel()).repeat(32)


def f64(x):
    return np.asarray(x).astype(np.float64)


def striped(idx):
    return np.tile(np.asarray(idx).reshape(-1, 16).T, (8, 1)).astype(np.uint16)


def unstriped(offs):
    return offs[:16].T.reshape(-1).astype(np.int64)


E2M1 = np.array([0.0, 0.5, 1.0, 1.5, 2.0, 3.0, 4.0, 6.0, -0.0, -0.5, -1.0, -1.5, -2.0, -3.0, -4.0, -6.0])


def pack_weight(w, fmt):
    k, n = w.shape
    w = f64(np.asarray(w, np.float32).astype(ml_dtypes.bfloat16)).reshape(k // 32, 32, n)
    amax = np.abs(w).max(1)
    if fmt == "e4m3":
        byte = np.frexp(amax)[1] - 1 + 127 - 7
    else:
        mant, ex = np.frexp(amax / 6.0)
        byte = np.where(mant > 0.5, ex, ex - 1) + 127
    byte = np.clip(np.where(amax > 0, byte, 1), 1, 254)
    scaled = (w * np.exp2(127.0 - byte)[:, None, :]).reshape(k, n).astype(np.float32)
    by_word = np.ascontiguousarray(scaled.reshape(k // 512, 128, 4, n).transpose(0, 1, 3, 2))
    if fmt == "e4m3":
        words = by_word.astype(ml_dtypes.float8_e4m3fn).view(np.uint8)
    else:
        c = by_word.astype(ml_dtypes.float4_e2m1fn).view(np.uint8) & 0xF
        words = (c[..., 0::2] | (c[..., 1::2] << 4)).reshape(k // 512, 128, 2 * n)
    return np.ascontiguousarray(words), np.ascontiguousarray(byte.astype(np.uint8).reshape(k // 512, 16, n))


def unpack_weight(words, scales, fmt):
    g, _, n = scales.shape
    words = np.ascontiguousarray(words).reshape(g, 128, n, -1)
    if fmt == "e4m3":
        vals = words.view(ml_dtypes.float8_e4m3fn).astype(np.float64)
    else:
        nib = np.empty((g, 128, n, 4), np.uint8)
        nib[..., 0::2] = words & 0xF
        nib[..., 1::2] = words >> 4
        vals = E2M1[nib]
    vals = vals * np.repeat(np.exp2(scales.astype(np.float64) - 127.0), 8, axis=1)[..., None]
    return vals.transpose(0, 1, 3, 2).reshape(g * 512, n)


def sigmoid(v):
    return 1.0 / (1.0 + np.exp(-v))


D, E, T, I, Q = 512, 512, 2048, 512, 128


def setup_inputs():
    n = np.random.standard_normal
    idx = np.random.permutation(T)[:I]
    fd = mx_kscale(D)
    fe = mx_kscale(E)
    keysp = pack_weight(n((D, T)) / fd[:, None], "e4m3")
    valsp = pack_weight(n((E, T)) / fe[:, None], "e4m3")
    return {
        "query": (n((D, Q)) * 0.8 / np.sqrt(D) * fd[:, None]).astype(np.float32),
        "keys_words": keysp[0],
        "keys_scales": keysp[1],
        "th": (np.random.uniform(0.4, 1.0, (Q, 1))).astype(np.float32),
        "gout": (n((E, Q)) * 1 / np.sqrt(E) * fe[:, None]).astype(np.float32),
        "vals_words": valsp[0],
        "vals_scales": valsp[1],
        "base": (0.5 * n((Q, I))).astype(np.float32),
        "offs": striped(idx),
    }


def reference(query, keys_words, keys_scales, th, gout, vals_words, vals_scales, base, offs):
    idx = unstriped(offs)
    keysu = unpack_weight(keys_words, keys_scales, "e4m3")
    valsu = unpack_weight(vals_words, vals_scales, "e4m3")
    queryq = mxq(f64(query), 0, "e4m3")
    keysidxg = keysu[:, idx]
    a = queryq.T @ keysidxg
    e1s = sigmoid((f64(th) - np.mean(np.square(a), axis=1, keepdims=True)) * 4.0)
    p = np.exp(a - np.max(a, axis=1, keepdims=True))
    z = np.sum(p, axis=1, keepdims=True)
    goutq = mxq(f64(gout), 0, "e4m3")
    valsidxg = valsu[:, idx]
    c0 = goutq.T @ valsidxg
    dz = np.sum(c0 * (1.0 - e1s) * p / np.square(z) * (-1.0), axis=1, keepdims=True)
    dp = c0 * (1.0 - e1s) / z + dz
    de1s = np.sum(c0, axis=1, keepdims=True) / 512.0 - np.sum(c0 * p / z, axis=1, keepdims=True)
    da = dp * p + de1s * e1s * (1.0 - e1s) * 4.0 * (-1.0) / 512.0 * a * 2.0
    hda = da * 512.0 * 2.0 * 512.0
    hde1s = np.sum(hda * 2.0 * a, axis=1, keepdims=True) / 512.0 * (-1.0) * 4.0 * (1.0 - e1s) * e1s
    hdp = hda * p
    hdz = np.sum(hdp, axis=1, keepdims=True)
    hz = np.sum(hde1s * (-1.0) * c0 * p / np.square(z) * (-1.0), axis=1, keepdims=True) + np.sum(hdp * c0 * (1.0 - e1s) / np.square(z) * (-1.0), axis=1, keepdims=True) + np.sum(hdz * (-1.0) * c0 * (1.0 - e1s) * p / np.square(np.square(z)) * (-1.0), axis=1, keepdims=True) * z * 2.0
    hp = hda * dp + hde1s * (-1.0) * c0 / z + hdz * (-1.0) / np.square(z) * c0 * (1.0 - e1s) + hz
    he1s = np.sum(hda * 2.0 * a, axis=1, keepdims=True) / 512.0 * (-1.0) * 4.0 * (1.0 - e1s) * de1s - np.sum(hda * 2.0 * a, axis=1, keepdims=True) / 512.0 * (-1.0) * 4.0 * de1s * e1s - np.sum(hdp / z * c0, axis=1, keepdims=True) - np.sum(hdz * (-1.0) / np.square(z) * p * c0, axis=1, keepdims=True)
    ha = hda * 2.0 * de1s * e1s * (1.0 - e1s) * 4.0 * (-1.0) / 512.0 + hp * p + he1s * e1s * (1.0 - e1s) * 4.0 * (-1.0) / 512.0 * a * 2.0
    y = ha + f64(base)
    return y

@@ -1,0 +1,187 @@
+from contextlib import ExitStack
+
+import concourse.mybir as mybir
+
+D, E, T, I, Q = 512, 512, 2048, 512, 128
+FLOPS = 2 * Q * I * (D + E)
+
+F32 = mybir.dt.float32
+BF16 = mybir.dt.bfloat16
+I32 = mybir.dt.int32
+U32 = mybir.dt.uint32
+U16 = mybir.dt.uint16
+U8 = mybir.dt.uint8
+FP8X4 = mybir.dt.float8_e4m3fn_x4
+ALU = mybir.AluOpType
+ACT = mybir.ActivationFunctionType
+
+P = 128
+PACK = 4
+HALF = I // 2
+ROOT_ALPHA = 2.0**8.5
+
+
+def tile_attend_gpevenbyspread_kernel(tc, query, keys_words, keys_scales, th, gout, vals_words, vals_scales, base, offs, out):
+    nc = tc.nc
+    halves = [slice(0, HALF), slice(HALF, I)]
+
+    with ExitStack() as ctx:
+        sb = ctx.enter_context(tc.tile_pool(name="sb", bufs=1))
+        ps = ctx.enter_context(tc.psum_pool(name="ps", bufs=1))
+
+        def col(name):
+            return sb.tile([P, 1], F32, name=name)
+
+        def wide(name):
+            return sb.tile([P, I], F32, name=name)
+
+        def fma(dst, x, scale, bias=0.0):
+            nc.scalar.activation(out=dst, in_=x, func=ACT.Identity, scale=scale, bias=bias)
+
+        offsets = sb.tile([P, I // 16], U16, name="offsets")
+        k_pool = sb.tile([P, T], I32, name="k_pool")
+        v_pool = sb.tile([P, T], I32, name="v_pool")
+        k_spool = sb.tile([P, T], U8, name="k_spool")
+        v_spool = sb.tile([P, T], U8, name="v_spool")
+        q_raw = sb.tile([P, PACK, Q], F32, name="q_raw")
+        g_raw = sb.tile([P, PACK, Q], F32, name="g_raw")
+        th_sb = col("th_sb")
+        base_sb = wide("base_sb")
+
+        nc.vector.memset(k_spool[:].bitcast(I32), 0)
+        nc.vector.memset(v_spool[:].bitcast(I32), 0)
+        zfac = sb.tile([P, 3], F32, name="zfac")
+        nc.vector.memset(zfac[:, 0:1], 1.0)
+        warm = col("warm")
+        nc.scalar.activation(out=warm[:], in_=zfac[:, 0:1], func=ACT.Exp)
+
+        def load_scales(queue, pool, src):
+            for quad in range(4):
+                queue.dma_start(out=pool[32 * quad : 32 * quad + 4, :].bitcast(I32), in_=src[0, 4 * quad : 4 * quad + 4, :].bitcast(I32))
+
+        def load_words(pool, src):
+            nc.sync.dma_start(out=pool[:], in_=src[0].rearrange("p n t -> p (n t)").bitcast(I32))
+
+        nc.sync.dma_start(offsets[:], offs)
+        nc.sync.dma_start(out=q_raw[:], in_=query.rearrange("(p j) w -> p j w", j=PACK))
+        load_scales(nc.sync, k_spool, keys_scales)
+        load_words(k_pool, keys_words)
+        nc.sync.dma_start(out=g_raw[:], in_=gout.rearrange("(p j) w -> p j w", j=PACK))
+        load_scales(nc.scalar, v_spool, vals_scales)
+        load_words(v_pool, vals_words)
+        nc.sync.dma_start(out=th_sb[:], in_=th)
+        nc.sync.dma_start(out=base_sb[:], in_=base)
+
+        def quantize(raw, name):
+            grouped = sb.tile([P, Q, PACK], BF16, name=name + "_bf", align_bytes=64)
+            codes = sb.tile([P, Q], U32, name=name + "_codes", align_bytes=64)
+            scales = sb.tile([P, Q], U8, name=name + "_scales", align_bytes=64)
+            nc.scalar.copy(out=grouped[:], in_=raw[:].rearrange("p j w -> p w j"))
+            nc.vector.quantize_mx(out=codes[:].bitcast(FP8X4), scales=scales[:], in_=grouped[:].rearrange("p w j -> p (w j)"))
+            return codes, scales
+
+        def gather_scales(pool, name):
+            picked = sb.tile([P, I], U8, name=name, align_bytes=64)
+            nc.vector.tensor_copy(picked[:], pool[:].indirect(offsets[:]))
+            return picked
+
+        def gather_multiply(pool, picked_scales, codes, scales, name):
+            picked = sb.tile([P, I], U32, name=name + "_words", align_bytes=64)
+            acc = ps.tile([P, I], F32, name=name + "_acc")
+            for h, cols in enumerate(halves):
+                nc.vector.tensor_copy(picked[:, cols], pool[:].bitcast(U32).indirect(offsets[:, 16 * h : 16 * (h + 1)]))
+            for cols in halves:
+                nc.tensor.matmul_mx(out=acc[:, cols], lhsT=codes[:].bitcast(FP8X4), lhsT_scale=scales[:],
+                                    rhs=picked[:, cols].bitcast(FP8X4), rhs_scale=picked_scales[:, cols], start=True, stop=True)
+            return acc
+
+        k_scales = gather_scales(k_spool, "k_scales")
+        q_codes, q_scales = quantize(q_raw, "q")
+        v_scales = gather_scales(v_spool, "v_scales")
+        a = gather_multiply(k_pool, k_scales, q_codes, q_scales, "a")
+        g_codes, g_scales = quantize(g_raw, "g")
+
+        th2 = col("th2")
+        fma(th2[:], th_sb[:], 2.0)
+
+        neg_a, neg_max = wide("neg_a"), col("neg_max")
+        nc.vector.tensor_scalar(out=neg_a[:], in0=a[:], scalar1=-1.0, scalar2=None, op0=ALU.mult, op1=ALU.min, accum_out=neg_max[:])
+        p, z = wide("p"), col("z")
+        nc.scalar.activation(out=p[:], in_=neg_a[:], func=ACT.Exp, scale=-1.0, bias=neg_max[:], accum_out=z[:])
+
+        c = gather_multiply(v_pool, v_scales, g_codes, g_scales, "c")
+
+        r = zfac[:, 2:3]
+        nc.vector.reciprocal(out=r, in_=z[:])
+        junk_v, junk_s = wide("junk_v"), wide("junk_s")
+        saw = col("saw")
+        nc.vector.scalar_tensor_tensor(out=junk_v[:], in0=a[:], scalar=r, in1=p[:], op0=ALU.mult, op1=ALU.mult, accum_out=saw[:])
+
+        p2, spp, s64 = wide("p2"), col("spp"), col("s64")
+        nc.scalar.activation(out=p2[:], in_=p[:], func=ACT.Square, accum_out=spp[:])
+        neg_r = col("neg_r")
+        fma(neg_r[:], r, -1.0)
+        nc.scalar.activation(out=junk_s[:], in_=neg_a[:], func=ACT.Square, scale=0.125, accum_out=s64[:])
+        tau = col("tau")
+        nc.scalar.activation(out=tau[:], in_=s64[:], func=ACT.Tanh, scale=-0.25, bias=th2[:])
+        r_spp, one_saw = col("r_spp"), col("one_saw")
+        fma(r_spp[:], spp[:], r)
+        fma(one_saw[:], saw[:], -1.0, 1.0)
+        sig, s, rho, nu1 = col("sig"), col("s"), col("rho"), col("nu1")
+        fma(sig[:], tau[:], 1.0 / 128, 1.0 / 128)
+        fma(s[:], tau[:], 0.5, 0.5)
+        fma(rho[:], tau[:], -ROOT_ALPHA, ROOT_ALPHA)
+        fma(zfac[:, 1:2], tau[:], 3.0 / 128, 1.0 / 128)
+        fma(nu1[:], tau[:], s64[:], 1.0)
+        kv = sb.tile([P, 4], F32, name="kv")
+        g2, rs, g0, sn = col("g2"), col("rs"), col("g0"), col("sn")
+        fma(g2[:], r, rho[:])
+        fma(rs[:], sig[:], rho[:])
+        fma(g0[:], s[:], s64[:], one_saw[:])
+        fma(sn[:], sig[:], nu1[:])
+        ar, asig, gh, pre3, pre4 = col("ar"), col("asig"), col("gh"), col("pre3"), col("pre4")
+        fma(asig[:], rs[:], rho[:])
+        fma(ar[:], g2[:], rho[:])
+        fma(gh[:], g2[:], 0.5)
+        fma(kv[:, 3:4], rs[:], 0.5)
+        fma(pre4[:], sn[:], asig[:])
+        fma(pre3[:], g0[:], kv[:, 3:4])
+
+        m, acc1n, delta, sta, stt = col("m"), col("acc1n"), col("delta"), col("sta"), col("stt")
+        t, ta = wide("t"), wide("ta")
+        junk_1, junk_2, junk_3 = wide("junk_1"), wide("junk_2"), wide("junk_3")
+        nc.vector.scalar_tensor_tensor(out=junk_1[:], in0=c[:], scalar=r, in1=p[:], op0=ALU.mult, op1=ALU.mult, accum_out=m[:])
+        nc.vector.scalar_tensor_tensor(out=junk_2[:], in0=c[:], scalar=neg_r[:], in1=p2[:], op0=ALU.mult, op1=ALU.mult, accum_out=acc1n[:])
+        nc.vector.scalar_tensor_tensor(out=t[:], in0=c[:], scalar=m[:], in1=p[:], op0=ALU.subtract, op1=ALU.mult)
+        nc.vector.tensor_scalar(out=junk_3[:], in0=c[:], scalar1=-1.0 / I, scalar2=m[:], op0=ALU.mult, op1=ALU.add, accum_out=delta[:])
+        nc.vector.scalar_tensor_tensor(out=ta[:], in0=t[:], scalar=r, in1=a[:], op0=ALU.mult, op1=ALU.mult, accum_out=sta[:])
+        nc.vector.tensor_scalar(out=kv[:, 0:3], in0=zfac[:], scalar1=asig[:], scalar2=delta[:], op0=ALU.mult, op1=ALU.mult)
+
+        nw1, x2a, d2, ad0a = col("nw1"), col("x2a"), col("d2"), col("ad0a")
+        ad = sb.tile([P, 3], F32, name="ad")
+        fma(nw1[:], m[:], r_spp[:], acc1n[:])
+        fma(x2a[:], nw1[:], gh[:])
+        junk_t = wide("junk_t")
+        nc.scalar.activation(out=junk_t[:], in_=t[:], func=ACT.Square, scale=r, accum_out=stt[:])
+        fma(d2[:], delta[:], delta[:])
+        fma(ad[:, 2:3], delta[:], pre3[:], x2a[:])
+        fma(ad0a[:], stt[:], asig[:])
+        fma(ad[:, 1:2], stt[:], ar[:])
+        fma(ad[:, 0:1], d2[:], pre4[:], ad0a[:])
+
+        coef = sb.tile([P, 3], F32, name="coef")
+        y0, y1, y2, sq, res = wide("y0"), wide("y1"), wide("y2"), wide("sq"), wide("res")
+        nc.vector.scalar_tensor_tensor(out=y0[:, halves[0]], in0=ta[:, halves[0]], scalar=kv[:, 0:1], in1=base_sb[:, halves[0]], op0=ALU.mult, op1=ALU.add)
+        nc.vector.scalar_tensor_tensor(out=coef[:], in0=kv[:, 1:4], scalar=sta[:], in1=ad[:], op0=ALU.mult, op1=ALU.add)
+        nc.vector.scalar_tensor_tensor(out=y0[:, halves[1]], in0=ta[:, halves[1]], scalar=kv[:, 0:1], in1=base_sb[:, halves[1]], op0=ALU.mult, op1=ALU.add)
+        b2 = col("b2")
+        fma(b2[:], coef[:, 2:3], coef[:, 2:3])
+        for cols in halves:
+            nc.scalar.activation(out=sq[:, cols], in_=t[:, cols], func=ACT.Square, scale=g2[:], bias=coef[:, 2:3])
+        for cols in halves:
+            nc.vector.scalar_tensor_tensor(out=y1[:, cols], in0=p[:, cols], scalar=coef[:, 1:2], in1=y0[:, cols], op0=ALU.mult, op1=ALU.subtract)
+        for cols in halves:
+            nc.vector.scalar_tensor_tensor(out=y2[:, cols], in0=a[:, cols], scalar=coef[:, 0:1], in1=y1[:, cols], op0=ALU.mult, op1=ALU.subtract)
+        for cols in halves:
+            nc.vector.scalar_tensor_tensor(out=res[:, cols], in0=sq[:, cols], scalar=b2[:], in1=y2[:, cols], op0=ALU.subtract, op1=ALU.add)
+            nc.sync.dma_start(out=out[:, cols], in_=res[:, cols])

@@ -40,9 +40,9 @@ def tile_attend_gpevenbyspread_kernel(tc, query, keys_words, keys_scales, th, go
 
         offsets = sb.tile([P, I // 16], U16, name="offsets")
         k_pool = sb.tile([P, T], I32, name="k_pool")
-        v_pool = sb.tile([P, T], I32, name="v_pool")
-        k_spool = sb.tile([P, T], U8, name="k_spool")
-        v_spool = sb.tile([P, T], U8, name="v_spool")
+        v_pool = sb.tile([P, T], I32, name="v_pool", tag="v_words")
+        k_spool = sb.tile([P, T], U8, name="k_spool", tag="k_bytes", align_bytes=64)
+        v_spool = sb.tile([P, T], U8, name="v_spool", tag="v_bytes")
         q_raw = sb.tile([P, PACK, Q], F32, name="q_raw")
         g_raw = sb.tile([P, PACK, Q], F32, name="g_raw")
         th_sb = col("th_sb")
@@ -50,31 +50,27 @@ def tile_attend_gpevenbyspread_kernel(tc, query, keys_words, keys_scales, th, go
 
         nc.vector.memset(k_spool[:].bitcast(I32), 0)
         nc.vector.memset(v_spool[:].bitcast(I32), 0)
-        zfac = sb.tile([P, 3], F32, name="zfac")
-        nc.vector.memset(zfac[:, 0:1], 1.0)
-        warm = col("warm")
-        nc.scalar.activation(out=warm[:], in_=zfac[:, 0:1], func=ACT.Exp)
 
-        def load_scales(queue, pool, src):
+        def load_scales(queues, pool, src):
             for quad in range(4):
-                queue.dma_start(out=pool[32 * quad : 32 * quad + 4, :].bitcast(I32), in_=src[0, 4 * quad : 4 * quad + 4, :].bitcast(I32))
+                queues[quad].dma_start(out=pool[32 * quad : 32 * quad + 4, :].bitcast(I32), in_=src[0, 4 * quad : 4 * quad + 4, :].bitcast(I32))
 
         def load_words(pool, src):
             nc.sync.dma_start(out=pool[:], in_=src[0].rearrange("p n t -> p (n t)").bitcast(I32))
 
         nc.sync.dma_start(offsets[:], offs)
         nc.sync.dma_start(out=q_raw[:], in_=query.rearrange("(p j) w -> p j w", j=PACK))
-        load_scales(nc.sync, k_spool, keys_scales)
+        load_scales([nc.sync, nc.sync, nc.scalar, nc.scalar], k_spool, keys_scales)
         load_words(k_pool, keys_words)
+        load_scales([nc.sync] * 4, v_spool, vals_scales)
         nc.sync.dma_start(out=g_raw[:], in_=gout.rearrange("(p j) w -> p j w", j=PACK))
-        load_scales(nc.scalar, v_spool, vals_scales)
         load_words(v_pool, vals_words)
         nc.sync.dma_start(out=th_sb[:], in_=th)
         nc.sync.dma_start(out=base_sb[:], in_=base)
 
-        def quantize(raw, name):
+        def quantize(raw, name, tag):
             grouped = sb.tile([P, Q, PACK], BF16, name=name + "_bf", align_bytes=64)
-            codes = sb.tile([P, Q], U32, name=name + "_codes", align_bytes=64)
+            codes = sb.tile([P, Q], U32, name=name + "_codes", tag=tag, align_bytes=64)
             scales = sb.tile([P, Q], U8, name=name + "_scales", align_bytes=64)
             nc.scalar.copy(out=grouped[:], in_=raw[:].rearrange("p j w -> p w j"))
             nc.vector.quantize_mx(out=codes[:].bitcast(FP8X4), scales=scales[:], in_=grouped[:].rearrange("p w j -> p (w j)"))
@@ -96,84 +92,89 @@ def tile_attend_gpevenbyspread_kernel(tc, query, keys_words, keys_scales, th, go
             return acc
 
         k_scales = gather_scales(k_spool, "k_scales")
-        q_codes, q_scales = quantize(q_raw, "q")
-        v_scales = gather_scales(v_spool, "v_scales")
+        q_codes, q_scales = quantize(q_raw, "q", "k_bytes")
         a = gather_multiply(k_pool, k_scales, q_codes, q_scales, "a")
-        g_codes, g_scales = quantize(g_raw, "g")
+        v_scales = gather_scales(v_spool, "v_scales")
+        g_codes, g_scales = quantize(g_raw, "g", "g_codes")
 
         th2 = col("th2")
-        fma(th2[:], th_sb[:], 2.0)
+        nc.gpsimd.tensor_scalar(out=th2[:], in0=th_sb[:], scalar1=2.0, scalar2=0.0, op0=ALU.mult, op1=ALU.add)
 
-        neg_a, neg_max = wide("neg_a"), col("neg_max")
+        neg_a, neg_max = sb.tile([P, I], F32, name="neg_a", tag="v_bytes"), col("neg_max")
         nc.vector.tensor_scalar(out=neg_a[:], in0=a[:], scalar1=-1.0, scalar2=None, op0=ALU.mult, op1=ALU.min, accum_out=neg_max[:])
         p, z = wide("p"), col("z")
         nc.scalar.activation(out=p[:], in_=neg_a[:], func=ACT.Exp, scale=-1.0, bias=neg_max[:], accum_out=z[:])
 
         c = gather_multiply(v_pool, v_scales, g_codes, g_scales, "c")
 
-        r = zfac[:, 2:3]
+        zfac = sb.tile([P, 2], F32, name="zfac", tag="v_words")
+        r = zfac[:, 1:2]
         nc.vector.reciprocal(out=r, in_=z[:])
-        junk_v, junk_s = wide("junk_v"), wide("junk_s")
-        saw = col("saw")
-        nc.vector.scalar_tensor_tensor(out=junk_v[:], in0=a[:], scalar=r, in1=p[:], op0=ALU.mult, op1=ALU.mult, accum_out=saw[:])
+        aw, saw = wide("aw"), col("saw")
+        nc.vector.scalar_tensor_tensor(out=aw[:], in0=a[:], scalar=r, in1=p[:], op0=ALU.mult, op1=ALU.mult, accum_out=saw[:])
 
-        p2, spp, s64 = wide("p2"), col("spp"), col("s64")
-        nc.scalar.activation(out=p2[:], in_=p[:], func=ACT.Square, accum_out=spp[:])
-        neg_r = col("neg_r")
-        fma(neg_r[:], r, -1.0)
+        junk_s, p2, spp, s64, tau = wide("junk_s"), wide("p2"), col("spp"), col("s64"), col("tau")
         nc.scalar.activation(out=junk_s[:], in_=neg_a[:], func=ACT.Square, scale=0.125, accum_out=s64[:])
-        tau = col("tau")
         nc.scalar.activation(out=tau[:], in_=s64[:], func=ACT.Tanh, scale=-0.25, bias=th2[:])
-        r_spp, one_saw = col("r_spp"), col("one_saw")
-        fma(r_spp[:], spp[:], r)
-        fma(one_saw[:], saw[:], -1.0, 1.0)
-        sig, s, rho, nu1 = col("sig"), col("s"), col("rho"), col("nu1")
+        nc.scalar.activation(out=p2[:], in_=p[:], func=ACT.Square, accum_out=spp[:])
+        sig, s, rho, rho4, nu1 = col("sig"), col("s"), col("rho"), col("rho4"), col("nu1")
+        r2, one_saw, spph = col("r2"), col("one_saw"), col("spph")
         fma(sig[:], tau[:], 1.0 / 128, 1.0 / 128)
-        fma(s[:], tau[:], 0.5, 0.5)
         fma(rho[:], tau[:], -ROOT_ALPHA, ROOT_ALPHA)
-        fma(zfac[:, 1:2], tau[:], 3.0 / 128, 1.0 / 128)
+        fma(r2[:], r, r)
+        fma(s[:], tau[:], 0.5, 0.5)
+        fma(rho4[:], tau[:], -ROOT_ALPHA / 4, ROOT_ALPHA / 4)
+        fma(zfac[:, 0:1], tau[:], 3.0 / 128, 1.0 / 128)
         fma(nu1[:], tau[:], s64[:], 1.0)
+        fma(one_saw[:], saw[:], -1.0, 1.0)
         kv = sb.tile([P, 4], F32, name="kv")
-        g2, rs, g0, sn = col("g2"), col("rs"), col("g0"), col("sn")
-        fma(g2[:], r, rho[:])
+        pre = sb.tile([P, 3], F32, name="pre")
+        asig = pre[:, 0:1]
+        g2, rs, g0, sn, n2r2 = col("g2"), col("rs"), col("g0"), col("sn"), col("n2r2")
         fma(rs[:], sig[:], rho[:])
-        fma(g0[:], s[:], s64[:], one_saw[:])
+        fma(n2r2[:], r2[:], -2.0)
+        fma(g2[:], r, rho[:])
+        fma(spph[:], spp[:], 0.5)
         fma(sn[:], sig[:], nu1[:])
-        ar, asig, gh, pre3, pre4 = col("ar"), col("asig"), col("gh"), col("pre3"), col("pre4")
-        fma(asig[:], rs[:], rho[:])
-        fma(ar[:], g2[:], rho[:])
-        fma(gh[:], g2[:], 0.5)
+        fma(g0[:], s[:], s64[:], one_saw[:])
+        ar, nghr, pre3, pre4 = col("ar"), col("nghr"), col("pre3"), col("pre4")
+        fma(asig, rs[:], rho[:])
         fma(kv[:, 3:4], rs[:], 0.5)
-        fma(pre4[:], sn[:], asig[:])
+        fma(ar[:], g2[:], rho[:])
+        fma(nghr[:], n2r2[:], rho4[:])
+        fma(pre[:, 1:3], zfac[:], asig)
+        fma(pre4[:], sn[:], asig)
         fma(pre3[:], g0[:], kv[:, 3:4])
 
-        m, acc1n, delta, sta, stt = col("m"), col("acc1n"), col("delta"), col("sta"), col("stt")
-        t, ta = wide("t"), wide("ta")
-        junk_1, junk_2, junk_3 = wide("junk_1"), wide("junk_2"), wide("junk_3")
-        nc.vector.scalar_tensor_tensor(out=junk_1[:], in0=c[:], scalar=r, in1=p[:], op0=ALU.mult, op1=ALU.mult, accum_out=m[:])
-        nc.vector.scalar_tensor_tensor(out=junk_2[:], in0=c[:], scalar=neg_r[:], in1=p2[:], op0=ALU.mult, op1=ALU.mult, accum_out=acc1n[:])
-        nc.vector.scalar_tensor_tensor(out=t[:], in0=c[:], scalar=m[:], in1=p[:], op0=ALU.subtract, op1=ALU.mult)
-        nc.vector.tensor_scalar(out=junk_3[:], in0=c[:], scalar1=-1.0 / I, scalar2=m[:], op0=ALU.mult, op1=ALU.add, accum_out=delta[:])
-        nc.vector.scalar_tensor_tensor(out=ta[:], in0=t[:], scalar=r, in1=a[:], op0=ALU.mult, op1=ALU.mult, accum_out=sta[:])
-        nc.vector.tensor_scalar(out=kv[:, 0:3], in0=zfac[:], scalar1=asig[:], scalar2=delta[:], op0=ALU.mult, op1=ALU.mult)
+        m, neg_mean, spt, delta, sta, swc2 = col("m"), col("neg_mean"), col("spt"), col("delta"), col("sta"), col("swc2")
+        t, ta, wc = wide("t"), wide("ta"), wide("wc")
+        junk_2, junk_3, junk_t = wide("junk_2"), wide("junk_3"), wide("junk_t")
+        nc.vector.scalar_tensor_tensor(out=wc[:], in0=c[:], scalar=r, in1=p[:], op0=ALU.mult, op1=ALU.mult, accum_out=m[:])
+        nc.vector.tensor_scalar(out=junk_3[:], in0=c[:], scalar1=-1.0 / I, scalar2=None, op0=ALU.mult, op1=ALU.add, accum_out=neg_mean[:])
+        nc.vector.scalar_tensor_tensor(out=junk_2[:], in0=c[:], scalar=m[:], in1=p2[:], op0=ALU.subtract, op1=ALU.mult, accum_out=spt[:])
+        nc.vector.scalar_tensor_tensor(out=ta[:], in0=c[:], scalar=m[:], in1=aw[:], op0=ALU.subtract, op1=ALU.mult, accum_out=sta[:])
 
-        nw1, x2a, d2, ad0a = col("nw1"), col("x2a"), col("d2"), col("ad0a")
+        n2mr2, d2, y0c, x2, u2, stt = col("n2mr2"), col("d2"), col("y0c"), col("x2"), col("u2"), col("stt")
         ad = sb.tile([P, 3], F32, name="ad")
-        fma(nw1[:], m[:], r_spp[:], acc1n[:])
-        fma(x2a[:], nw1[:], gh[:])
-        junk_t = wide("junk_t")
-        nc.scalar.activation(out=junk_t[:], in_=t[:], func=ACT.Square, scale=r, accum_out=stt[:])
+        nc.scalar.activation(out=junk_t[:], in_=wc[:], func=ACT.Square, accum_out=swc2[:])
+        fma(delta[:], neg_mean[:], 1.0, m[:])
+        fma(n2mr2[:], m[:], n2r2[:])
+        nc.vector.tensor_scalar(out=kv[:, 0:3], in0=pre[:], scalar1=delta[:], scalar2=None, op0=ALU.mult)
+        nc.vector.scalar_tensor_tensor(out=t[:], in0=c[:], scalar=m[:], in1=p[:], op0=ALU.subtract, op1=ALU.mult)
         fma(d2[:], delta[:], delta[:])
-        fma(ad[:, 2:3], delta[:], pre3[:], x2a[:])
-        fma(ad0a[:], stt[:], asig[:])
+        fma(x2[:], delta[:], pre3[:])
+        fma(u2[:], m[:], spph[:], spt[:])
+        fma(y0c[:], d2[:], pre4[:])
+        fma(ad[:, 2:3], spt[:], nghr[:], x2[:])
+        fma(stt[:], u2[:], n2mr2[:], swc2[:])
+        fma(ad[:, 0:1], stt[:], asig, y0c[:])
         fma(ad[:, 1:2], stt[:], ar[:])
-        fma(ad[:, 0:1], d2[:], pre4[:], ad0a[:])
 
         coef = sb.tile([P, 3], F32, name="coef")
         y0, y1, y2, sq, res = wide("y0"), wide("y1"), wide("y2"), wide("sq"), wide("res")
-        nc.vector.scalar_tensor_tensor(out=y0[:, halves[0]], in0=ta[:, halves[0]], scalar=kv[:, 0:1], in1=base_sb[:, halves[0]], op0=ALU.mult, op1=ALU.add)
         nc.vector.scalar_tensor_tensor(out=coef[:], in0=kv[:, 1:4], scalar=sta[:], in1=ad[:], op0=ALU.mult, op1=ALU.add)
-        nc.vector.scalar_tensor_tensor(out=y0[:, halves[1]], in0=ta[:, halves[1]], scalar=kv[:, 0:1], in1=base_sb[:, halves[1]], op0=ALU.mult, op1=ALU.add)
+        for cols in halves:
+            nc.vector.scalar_tensor_tensor(out=y0[:, cols], in0=ta[:, cols], scalar=kv[:, 0:1], in1=base_sb[:, cols], op0=ALU.mult, op1=ALU.add)
         b2 = col("b2")
         fma(b2[:], coef[:, 2:3], coef[:, 2:3])
         for cols in halves:
@@ -182,6 +183,6 @@ def tile_attend_gpevenbyspread_kernel(tc, query, keys_words, keys_scales, th, go
             nc.vector.scalar_tensor_tensor(out=y1[:, cols], in0=p[:, cols], scalar=coef[:, 1:2], in1=y0[:, cols], op0=ALU.mult, op1=ALU.subtract)
         for cols in halves:
             nc.vector.scalar_tensor_tensor(out=y2[:, cols], in0=a[:, cols], scalar=coef[:, 0:1], in1=y1[:, cols], op0=ALU.mult, op1=ALU.subtract)
-        for cols in halves:
+        for cols, queue in zip(halves, (nc.sync, nc.scalar)):
             nc.vector.scalar_tensor_tensor(out=res[:, cols], in0=sq[:, cols], scalar=b2[:], in1=y2[:, cols], op0=ALU.subtract, op1=ALU.add)
-            nc.sync.dma_start(out=out[:, cols], in_=res[:, cols])
+            queue.dma_start(out=out[:, cols], in_=res[:, cols])

@@ -39,7 +39,7 @@ def tile_attend_gpevenbyspread_kernel(tc, query, keys_words, keys_scales, th, go
             nc.scalar.activation(out=dst, in_=x, func=ACT.Identity, scale=scale, bias=bias)
 
         offsets = sb.tile([P, I // 16], U16, name="offsets")
-        k_pool = sb.tile([P, T], I32, name="k_pool")
+        k_pool = sb.tile([P, T], I32, name="k_pool", tag="k_words", align_bytes=64)
         v_pool = sb.tile([P, T], I32, name="v_pool", tag="v_words")
         k_spool = sb.tile([P, T], U8, name="k_spool", tag="k_bytes", align_bytes=64)
         v_spool = sb.tile([P, T], U8, name="v_spool", tag="v_bytes")
@@ -49,20 +49,20 @@ def tile_attend_gpevenbyspread_kernel(tc, query, keys_words, keys_scales, th, go
         base_sb = wide("base_sb")
 
         nc.vector.memset(k_spool[:].bitcast(I32), 0)
-        nc.vector.memset(v_spool[:].bitcast(I32), 0)
+        nc.gpsimd.memset(v_spool[:].bitcast(I32), 0)
 
-        def load_scales(queues, pool, src):
-            for quad in range(4):
-                queues[quad].dma_start(out=pool[32 * quad : 32 * quad + 4, :].bitcast(I32), in_=src[0, 4 * quad : 4 * quad + 4, :].bitcast(I32))
+        def load_scales(queues, pool, first, src):
+            for j in range(4):
+                queues[j].dma_start(out=pool[first + j : P : 32, :].bitcast(I32), in_=src[0, j:16:4, :].bitcast(I32))
 
         def load_words(pool, src):
             nc.sync.dma_start(out=pool[:], in_=src[0].rearrange("p n t -> p (n t)").bitcast(I32))
 
         nc.sync.dma_start(offsets[:], offs)
         nc.sync.dma_start(out=q_raw[:], in_=query.rearrange("(p j) w -> p j w", j=PACK))
-        load_scales([nc.sync, nc.sync, nc.scalar, nc.scalar], k_spool, keys_scales)
+        load_scales([nc.sync, nc.sync, nc.scalar, nc.scalar], k_spool, 0, keys_scales)
         load_words(k_pool, keys_words)
-        load_scales([nc.sync] * 4, v_spool, vals_scales)
+        load_scales([nc.gpsimd] * 4, v_spool, 4, vals_scales)
         nc.sync.dma_start(out=g_raw[:], in_=gout.rearrange("(p j) w -> p j w", j=PACK))
         load_words(v_pool, vals_words)
         nc.sync.dma_start(out=th_sb[:], in_=th)
@@ -76,25 +76,25 @@ def tile_attend_gpevenbyspread_kernel(tc, query, keys_words, keys_scales, th, go
             nc.vector.quantize_mx(out=codes[:].bitcast(FP8X4), scales=scales[:], in_=grouped[:].rearrange("p w j -> p (w j)"))
             return codes, scales
 
-        def gather_scales(pool, name):
-            picked = sb.tile([P, I], U8, name=name, align_bytes=64)
+        def gather_scales(pool, name, tag):
+            picked = sb.tile([P, I], U8, name=name, tag=tag, align_bytes=64)
             nc.vector.tensor_copy(picked[:], pool[:].indirect(offsets[:]))
             return picked
 
-        def gather_multiply(pool, picked_scales, codes, scales, name):
+        def gather_multiply(pool, picked_scales, first, codes, scales, name):
             picked = sb.tile([P, I], U32, name=name + "_words", align_bytes=64)
             acc = ps.tile([P, I], F32, name=name + "_acc")
             for h, cols in enumerate(halves):
                 nc.vector.tensor_copy(picked[:, cols], pool[:].bitcast(U32).indirect(offsets[:, 16 * h : 16 * (h + 1)]))
             for cols in halves:
                 nc.tensor.matmul_mx(out=acc[:, cols], lhsT=codes[:].bitcast(FP8X4), lhsT_scale=scales[:],
-                                    rhs=picked[:, cols].bitcast(FP8X4), rhs_scale=picked_scales[:, cols], start=True, stop=True)
+                                    rhs=picked[:, cols].bitcast(FP8X4), rhs_scale=picked_scales[first:P, cols], start=True, stop=True)
             return acc
 
-        k_scales = gather_scales(k_spool, "k_scales")
+        k_scales = gather_scales(k_spool, "k_scales", "k_scales")
         q_codes, q_scales = quantize(q_raw, "q", "k_bytes")
-        a = gather_multiply(k_pool, k_scales, q_codes, q_scales, "a")
-        v_scales = gather_scales(v_spool, "v_scales")
+        a = gather_multiply(k_pool, k_scales, 0, q_codes, q_scales, "a")
+        v_scales = gather_scales(v_spool, "v_scales", "k_words")
         g_codes, g_scales = quantize(g_raw, "g", "g_codes")
 
         th2 = col("th2")
@@ -105,7 +105,7 @@ def tile_attend_gpevenbyspread_kernel(tc, query, keys_words, keys_scales, th, go
         p, z = wide("p"), col("z")
         nc.scalar.activation(out=p[:], in_=neg_a[:], func=ACT.Exp, scale=-1.0, bias=neg_max[:], accum_out=z[:])
 
-        c = gather_multiply(v_pool, v_scales, g_codes, g_scales, "c")
+        c = gather_multiply(v_pool, v_scales, 4, g_codes, g_scales, "c")
 
         zfac = sb.tile([P, 2], F32, name="zfac", tag="v_words")
         r = zfac[:, 1:2]

@@ -17,20 +17,22 @@ ACT = mybir.ActivationFunctionType
 
 P = 128
 PACK = 4
-HALF = I // 2
-ROOT_ALPHA = 2.0**8.5
+BLOCKS = 16
+LIST_ROWS = 16
+RHO_SCALE = 2.0**8.5
+KEYS_FIRST, VALS_FIRST = 0, 4
+HALVES = (slice(0, I // 2), slice(I // 2, I))
 
 
 def tile_attend_gpevenbyspread_kernel(tc, query, keys_words, keys_scales, th, gout, vals_words, vals_scales, base, offs, out):
     nc = tc.nc
-    halves = [slice(0, HALF), slice(HALF, I)]
 
     with ExitStack() as ctx:
         sb = ctx.enter_context(tc.tile_pool(name="sb", bufs=1))
         ps = ctx.enter_context(tc.psum_pool(name="ps", bufs=1))
 
-        def col(name):
-            return sb.tile([P, 1], F32, name=name)
+        def col(name, width=1):
+            return sb.tile([P, width], F32, name=name)
 
         def wide(name):
             return sb.tile([P, I], F32, name=name)
@@ -38,151 +40,183 @@ def tile_attend_gpevenbyspread_kernel(tc, query, keys_words, keys_scales, th, go
         def fma(dst, x, scale, bias=0.0):
             nc.scalar.activation(out=dst, in_=x, func=ACT.Identity, scale=scale, bias=bias)
 
-        offsets = sb.tile([P, I // 16], U16, name="offsets")
-        k_pool = sb.tile([P, T], I32, name="k_pool", tag="k_words", align_bytes=64)
-        v_pool = sb.tile([P, T], I32, name="v_pool", tag="v_words")
-        k_spool = sb.tile([P, T], U8, name="k_spool", tag="k_bytes", align_bytes=64)
-        v_spool = sb.tile([P, T], U8, name="v_spool", tag="v_bytes")
+        def stt(dst, x, scalar, op0, y, op1, total=None):
+            nc.vector.scalar_tensor_tensor(out=dst, in0=x, scalar=scalar, in1=y, op0=op0, op1=op1, accum_out=total)
+
+        offsets = sb.tile([P, I // LIST_ROWS], U16, name="offsets")
+        k_word_pool = sb.tile([P, T], I32, name="k_word_pool")
+        v_word_pool = sb.tile([P, T], I32, name="v_word_pool", tag="v_words")
+        k_byte_pool = sb.tile([P, T], U8, name="k_byte_pool", tag="k_bytes", align_bytes=64)
+        v_byte_pool = sb.tile([P, T], U8, name="v_byte_pool", tag="v_bytes")
         q_raw = sb.tile([P, PACK, Q], F32, name="q_raw")
         g_raw = sb.tile([P, PACK, Q], F32, name="g_raw")
-        th_sb = col("th_sb")
-        base_sb = wide("base_sb")
+        th_sb, base_sb = col("th_sb"), wide("base_sb")
 
-        nc.vector.memset(k_spool[:].bitcast(I32), 0)
-        nc.gpsimd.memset(v_spool[:].bitcast(I32), 0)
+        nc.vector.memset(k_byte_pool[:].bitcast(I32), 0)
+        nc.vector.memset(v_byte_pool[:].bitcast(I32), 0)
 
-        def load_scales(queues, pool, first, src):
+        def load_scale_bytes(queues, pool, first, src):
             for j in range(4):
-                queues[j].dma_start(out=pool[first + j : P : 32, :].bitcast(I32), in_=src[0, j:16:4, :].bitcast(I32))
+                queues[j].dma_start(out=pool[first + j : P : 32, :].bitcast(I32), in_=src[0, j:BLOCKS:4, :].bitcast(I32))
 
         def load_words(pool, src):
             nc.sync.dma_start(out=pool[:], in_=src[0].rearrange("p n t -> p (n t)").bitcast(I32))
 
+        def load_rows(raw, src):
+            nc.sync.dma_start(out=raw[:], in_=src.rearrange("(p j) w -> p j w", j=PACK))
+
         nc.sync.dma_start(offsets[:], offs)
-        nc.sync.dma_start(out=q_raw[:], in_=query.rearrange("(p j) w -> p j w", j=PACK))
-        load_scales([nc.sync, nc.sync, nc.scalar, nc.scalar], k_spool, 0, keys_scales)
-        load_words(k_pool, keys_words)
-        load_scales([nc.gpsimd] * 4, v_spool, 4, vals_scales)
-        nc.sync.dma_start(out=g_raw[:], in_=gout.rearrange("(p j) w -> p j w", j=PACK))
-        load_words(v_pool, vals_words)
+        load_rows(q_raw, query)
+        load_scale_bytes([nc.sync, nc.sync, nc.scalar, nc.scalar], k_byte_pool, KEYS_FIRST, keys_scales)
+        load_words(k_word_pool, keys_words)
+        load_scale_bytes([nc.sync] * 4, v_byte_pool, VALS_FIRST, vals_scales)
+        load_rows(g_raw, gout)
+        load_words(v_word_pool, vals_words)
         nc.sync.dma_start(out=th_sb[:], in_=th)
         nc.sync.dma_start(out=base_sb[:], in_=base)
 
-        def quantize(raw, name, tag):
-            grouped = sb.tile([P, Q, PACK], BF16, name=name + "_bf", align_bytes=64)
-            codes = sb.tile([P, Q], U32, name=name + "_codes", tag=tag, align_bytes=64)
+        def quantize(raw, name, codes_tag):
+            grouped = sb.tile([P, Q, PACK], BF16, name=name + "_bf16", align_bytes=64)
+            codes = sb.tile([P, Q], U32, name=name + "_codes", tag=codes_tag, align_bytes=64)
             scales = sb.tile([P, Q], U8, name=name + "_scales", align_bytes=64)
             nc.scalar.copy(out=grouped[:], in_=raw[:].rearrange("p j w -> p w j"))
             nc.vector.quantize_mx(out=codes[:].bitcast(FP8X4), scales=scales[:], in_=grouped[:].rearrange("p w j -> p (w j)"))
             return codes, scales
 
-        def gather_scales(pool, name, tag):
-            picked = sb.tile([P, I], U8, name=name, tag=tag, align_bytes=64)
+        def gather_bytes(pool, name):
+            picked = sb.tile([P, I], U8, name=name, align_bytes=64)
             nc.vector.tensor_copy(picked[:], pool[:].indirect(offsets[:]))
             return picked
 
-        def gather_multiply(pool, picked_scales, first, codes, scales, name):
-            picked = sb.tile([P, I], U32, name=name + "_words", align_bytes=64)
-            acc = ps.tile([P, I], F32, name=name + "_acc")
-            for h, cols in enumerate(halves):
-                nc.vector.tensor_copy(picked[:, cols], pool[:].bitcast(U32).indirect(offsets[:, 16 * h : 16 * (h + 1)]))
-            for cols in halves:
-                nc.tensor.matmul_mx(out=acc[:, cols], lhsT=codes[:].bitcast(FP8X4), lhsT_scale=scales[:],
-                                    rhs=picked[:, cols].bitcast(FP8X4), rhs_scale=picked_scales[first:P, cols], start=True, stop=True)
-            return acc
+        def gather_words(pool, name):
+            picked = sb.tile([P, I], U32, name=name, align_bytes=64)
+            for cols in HALVES:
+                entries = offsets[:, cols.start // LIST_ROWS : cols.stop // LIST_ROWS]
+                nc.vector.tensor_copy(picked[:, cols], pool[:].bitcast(U32).indirect(entries))
+            return picked
 
-        k_scales = gather_scales(k_spool, "k_scales", "k_scales")
-        q_codes, q_scales = quantize(q_raw, "q", "k_bytes")
-        a = gather_multiply(k_pool, k_scales, 0, q_codes, q_scales, "a")
-        v_scales = gather_scales(v_spool, "v_scales", "k_words")
-        g_codes, g_scales = quantize(g_raw, "g", "g_codes")
+        def multiply(acc, stationary, words, scale_bytes, first, cols):
+            codes, scales = stationary
+            nc.tensor.matmul_mx(
+                out=acc, lhsT=codes[:].bitcast(FP8X4), lhsT_scale=scales[:],
+                rhs=words[:, cols].bitcast(FP8X4), rhs_scale=scale_bytes[first:P, cols], start=True, stop=True,
+            )
 
-        th2 = col("th2")
-        nc.gpsimd.tensor_scalar(out=th2[:], in0=th_sb[:], scalar1=2.0, scalar2=0.0, op0=ALU.mult, op1=ALU.add)
+        k_bytes = gather_bytes(k_byte_pool, "k_bytes_picked")
+        q_mx = quantize(q_raw, "q", "k_bytes")
+        k_words = gather_words(k_word_pool, "k_words_picked")
+        a = ps.tile([P, I], F32, name="a")
+        for cols in HALVES:
+            multiply(a[:, cols], q_mx, k_words, k_bytes, KEYS_FIRST, cols)
+        v_bytes = gather_bytes(v_byte_pool, "v_bytes_picked")
+        g_mx = quantize(g_raw, "g", "g_codes")
 
         neg_a, neg_max = sb.tile([P, I], F32, name="neg_a", tag="v_bytes"), col("neg_max")
         nc.vector.tensor_scalar(out=neg_a[:], in0=a[:], scalar1=-1.0, scalar2=None, op0=ALU.mult, op1=ALU.min, accum_out=neg_max[:])
         p, z = wide("p"), col("z")
         nc.scalar.activation(out=p[:], in_=neg_a[:], func=ACT.Exp, scale=-1.0, bias=neg_max[:], accum_out=z[:])
 
-        c = gather_multiply(v_pool, v_scales, 4, g_codes, g_scales, "c")
+        v_words = gather_words(v_word_pool, "v_words_picked")
+        c = ps.tile([P, I], F32, name="c")
+        for cols in HALVES:
+            multiply(c[:, cols], g_mx, v_words, v_bytes, VALS_FIRST, cols)
+        c_again = ps.tile([P, I // 2], F32, name="c_again")
+        multiply(c_again[:], g_mx, v_words, v_bytes, VALS_FIRST, HALVES[0])
 
-        zfac = sb.tile([P, 2], F32, name="zfac", tag="v_words")
-        r = zfac[:, 1:2]
+        factors = sb.tile([P, 2], F32, name="factors", tag="v_words")
+        r = factors[:, 1:2]
         nc.vector.reciprocal(out=r, in_=z[:])
-        aw, saw = wide("aw"), col("saw")
-        nc.vector.scalar_tensor_tensor(out=aw[:], in0=a[:], scalar=r, in1=p[:], op0=ALU.mult, op1=ALU.mult, accum_out=saw[:])
+        aw, s_aw = wide("aw"), col("s_aw")
+        stt(aw[:], a[:], r, ALU.mult, p[:], ALU.mult, s_aw[:])
 
-        junk_s, p2, spp, s64, tau = wide("junk_s"), wide("p2"), col("spp"), col("s64"), col("tau")
-        nc.scalar.activation(out=junk_s[:], in_=neg_a[:], func=ACT.Square, scale=0.125, accum_out=s64[:])
-        nc.scalar.activation(out=tau[:], in_=s64[:], func=ACT.Tanh, scale=-0.25, bias=th2[:])
-        nc.scalar.activation(out=p2[:], in_=p[:], func=ACT.Square, accum_out=spp[:])
-        sig, s, rho, rho4, nu1 = col("sig"), col("s"), col("rho"), col("rho4"), col("nu1")
-        r2, one_saw, spph = col("r2"), col("one_saw"), col("spph")
-        fma(sig[:], tau[:], 1.0 / 128, 1.0 / 128)
-        fma(rho[:], tau[:], -ROOT_ALPHA, ROOT_ALPHA)
-        fma(r2[:], r, r)
+        a_sq, s_aa64, tau, pp, s_pp = wide("a_sq"), col("s_aa64"), col("tau"), wide("pp"), col("s_pp")
+        nc.scalar.activation(out=a_sq[:], in_=neg_a[:], func=ACT.Square, scale=0.125, accum_out=s_aa64[:])
+        th2 = col("th2")
+        fma(th2[:], th_sb[:], 2.0)
+        nc.scalar.activation(out=tau[:], in_=s_aa64[:], func=ACT.Tanh, scale=-2.0 * 64 / I, bias=th2[:])
+        nc.scalar.activation(out=pp[:], in_=p[:], func=ACT.Square, accum_out=s_pp[:])
+
+        sigma, rho, rr, s, rho4, one_nu, one_aw = (col(n) for n in ("sigma", "rho", "rr", "s", "rho4", "one_nu", "one_aw"))
+        fma(sigma[:], tau[:], 1.0 / 128, 1.0 / 128)
+        fma(rho[:], tau[:], -RHO_SCALE, RHO_SCALE)
+        fma(rr[:], r, r)
         fma(s[:], tau[:], 0.5, 0.5)
-        fma(rho4[:], tau[:], -ROOT_ALPHA / 4, ROOT_ALPHA / 4)
-        fma(zfac[:, 0:1], tau[:], 3.0 / 128, 1.0 / 128)
-        fma(nu1[:], tau[:], s64[:], 1.0)
-        fma(one_saw[:], saw[:], -1.0, 1.0)
-        kv = sb.tile([P, 4], F32, name="kv")
-        pre = sb.tile([P, 3], F32, name="pre")
-        asig = pre[:, 0:1]
-        g2, rs, g0, sn, n2r2 = col("g2"), col("rs"), col("g0"), col("sn"), col("n2r2")
-        fma(rs[:], sig[:], rho[:])
-        fma(n2r2[:], r2[:], -2.0)
-        fma(g2[:], r, rho[:])
-        fma(spph[:], spp[:], 0.5)
-        fma(sn[:], sig[:], nu1[:])
-        fma(g0[:], s[:], s64[:], one_saw[:])
-        ar, nghr, pre3, pre4 = col("ar"), col("nghr"), col("pre3"), col("pre4")
-        fma(asig, rs[:], rho[:])
-        fma(kv[:, 3:4], rs[:], 0.5)
-        fma(ar[:], g2[:], rho[:])
-        fma(nghr[:], n2r2[:], rho4[:])
-        fma(pre[:, 1:3], zfac[:], asig)
-        fma(pre4[:], sn[:], asig)
-        fma(pre3[:], g0[:], kv[:, 3:4])
+        fma(rho4[:], tau[:], -RHO_SCALE / 4, RHO_SCALE / 4)
+        fma(factors[:, 0:1], tau[:], 3.0 / 128, 1.0 / 128)
+        fma(one_nu[:], tau[:], s_aa64[:], 1.0)
+        fma(one_aw[:], s_aw[:], -1.0, 1.0)
 
-        m, neg_mean, spt, delta, sta, swc2 = col("m"), col("neg_mean"), col("spt"), col("delta"), col("sta"), col("swc2")
-        t, ta, wc = wide("t"), wide("ta"), wide("wc")
-        junk_2, junk_3, junk_t = wide("junk_2"), wide("junk_3"), wide("junk_t")
-        nc.vector.scalar_tensor_tensor(out=wc[:], in0=c[:], scalar=r, in1=p[:], op0=ALU.mult, op1=ALU.mult, accum_out=m[:])
-        nc.vector.tensor_scalar(out=junk_3[:], in0=c[:], scalar1=-1.0 / I, scalar2=None, op0=ALU.mult, op1=ALU.add, accum_out=neg_mean[:])
-        nc.vector.scalar_tensor_tensor(out=junk_2[:], in0=c[:], scalar=m[:], in1=p2[:], op0=ALU.subtract, op1=ALU.mult, accum_out=spt[:])
-        nc.vector.scalar_tensor_tensor(out=ta[:], in0=c[:], scalar=m[:], in1=aw[:], op0=ALU.subtract, op1=ALU.mult, accum_out=sta[:])
+        rho_sigma, neg2rr, rho_r, sigma_nu, kappa_in_c1 = (
+            col(n) for n in ("rho_sigma", "neg2rr", "rho_r", "sigma_nu", "kappa_in_c1")
+        )
+        neg_pp = col("neg_pp", 2)
+        fma(rho_sigma[:], sigma[:], rho[:])
+        fma(neg2rr[:], rr[:], -2.0)
+        fma(rho_r[:], r, rho[:])
+        fma(neg_pp[:, 0:1], s_pp[:], -0.5)
+        fma(neg_pp[:, 1:2], s_pp[:], -1.0)
+        fma(sigma_nu[:], sigma[:], one_nu[:])
+        fma(kappa_in_c1[:], s[:], s_aa64[:], one_aw[:])
 
-        n2mr2, d2, y0c, x2, u2, stt = col("n2mr2"), col("d2"), col("y0c"), col("x2"), col("u2"), col("stt")
-        ad = sb.tile([P, 3], F32, name="ad")
-        nc.scalar.activation(out=junk_t[:], in_=wc[:], func=ACT.Square, accum_out=swc2[:])
-        fma(delta[:], neg_mean[:], 1.0, m[:])
-        fma(n2mr2[:], m[:], n2r2[:])
-        nc.vector.tensor_scalar(out=kv[:, 0:3], in0=pre[:], scalar1=delta[:], scalar2=None, op0=ALU.mult)
-        nc.vector.scalar_tensor_tensor(out=t[:], in0=c[:], scalar=m[:], in1=p[:], op0=ALU.subtract, op1=ALU.mult)
-        fma(d2[:], delta[:], delta[:])
-        fma(x2[:], delta[:], pre3[:])
-        fma(u2[:], m[:], spph[:], spt[:])
-        fma(y0c[:], d2[:], pre4[:])
-        fma(ad[:, 2:3], spt[:], nghr[:], x2[:])
-        fma(stt[:], u2[:], n2mr2[:], swc2[:])
-        fma(ad[:, 0:1], stt[:], asig, y0c[:])
-        fma(ad[:, 1:2], stt[:], ar[:])
+        per_delta = col("per_delta", 3)
+        alpha_sigma = per_delta[:, 0:1]
+        half_rho_sigma, alpha_r, shift_pt, c3_dd, shift_d = (
+            col(n) for n in ("half_rho_sigma", "alpha_r", "shift_pt", "c3_dd", "shift_d")
+        )
+        fma(alpha_sigma, rho_sigma[:], rho[:])
+        fma(half_rho_sigma[:], rho_sigma[:], 0.5)
+        fma(alpha_r[:], rho_r[:], rho[:])
+        fma(shift_pt[:], neg2rr[:], rho4[:])
+        fma(per_delta[:, 1:3], factors[:], alpha_sigma)
+        fma(c3_dd[:], sigma_nu[:], alpha_sigma)
+        fma(shift_d[:], kappa_in_c1[:], half_rho_sigma[:])
 
-        coef = sb.tile([P, 3], F32, name="coef")
-        y0, y1, y2, sq, res = wide("y0"), wide("y1"), wide("y2"), wide("sq"), wide("res")
-        nc.vector.scalar_tensor_tensor(out=coef[:], in0=kv[:, 1:4], scalar=sta[:], in1=ad[:], op0=ALU.mult, op1=ALU.add)
-        for cols in halves:
-            nc.vector.scalar_tensor_tensor(out=y0[:, cols], in0=ta[:, cols], scalar=kv[:, 0:1], in1=base_sb[:, cols], op0=ALU.mult, op1=ALU.add)
-        b2 = col("b2")
-        fma(b2[:], coef[:, 2:3], coef[:, 2:3])
-        for cols in halves:
-            nc.scalar.activation(out=sq[:, cols], in_=t[:, cols], func=ACT.Square, scale=g2[:], bias=coef[:, 2:3])
-        for cols in halves:
-            nc.vector.scalar_tensor_tensor(out=y1[:, cols], in0=p[:, cols], scalar=coef[:, 1:2], in1=y0[:, cols], op0=ALU.mult, op1=ALU.subtract)
-        for cols in halves:
-            nc.vector.scalar_tensor_tensor(out=y2[:, cols], in0=a[:, cols], scalar=coef[:, 0:1], in1=y1[:, cols], op0=ALU.mult, op1=ALU.subtract)
-        for cols, queue in zip(halves, (nc.sync, nc.scalar)):
-            nc.vector.scalar_tensor_tensor(out=res[:, cols], in0=sq[:, cols], scalar=b2[:], in1=y2[:, cols], op0=ALU.subtract, op1=ALU.add)
-            queue.dma_start(out=out[:, cols], in_=res[:, cols])
+        wc, m = wide("wc"), col("m")
+        c_scaled, delta, mean_0, mean_1 = wide("c_scaled"), col("delta"), col("mean_0"), col("mean_1")
+        nc.scalar.activation(out=c_scaled[:, HALVES[0]], in_=c_again[:], func=ACT.Identity, scale=-1.0 / I, accum_out=mean_0[:])
+        ppc, s_ppc = wide("ppc"), col("s_ppc")
+        ta, s_ta = wide("ta"), col("s_ta")
+        pc = wide("pc")
+        stt(wc[:], c[:], r, ALU.mult, p[:], ALU.mult, m[:])
+        stt(ppc[:], c[:], 1.0, ALU.mult, pp[:], ALU.mult, s_ppc[:])
+        nc.vector.tensor_scalar(out=c_scaled[:, HALVES[1]], in0=c[:, HALVES[1]], scalar1=-1.0 / I, scalar2=m[:], op0=ALU.mult, op1=ALU.add, accum_out=mean_1[:])
+        stt(ta[:], c[:], m[:], ALU.subtract, aw[:], ALU.mult, s_ta[:])
+        stt(pc[:], c[:], m[:], ALU.subtract, p[:], ALU.mult)
+
+        wc_sq, s_wcwc = wide("wc_sq"), col("s_wcwc")
+        nc.scalar.activation(out=wc_sq[:], in_=wc[:], func=ACT.Square, accum_out=s_wcwc[:])
+        neg2mrr, dd, shift_0, shift_1, c3_0, c3_1, c2_0 = (
+            col(n) for n in ("neg2mrr", "dd", "shift_0", "shift_1", "c3_0", "c3_1", "c2_0")
+        )
+        shift, shift_sq, coef_a, coef_p = (col(n) for n in ("shift", "shift_sq", "coef_a", "coef_p"))
+        s_tt = col("s_tt")
+        centred = col("centred", 2)
+        by_delta = col("by_delta", 3)
+        fma(neg2mrr[:], m[:], neg2rr[:])
+        fma(centred[:], neg_pp[:], m[:], s_ppc[:])
+        fma(delta[:], mean_1[:], 1.0, mean_0[:])
+        fma(s_tt[:], centred[:, 0:1], neg2mrr[:], s_wcwc[:])
+        fma(shift_0[:], centred[:, 1:2], shift_pt[:])
+        fma(by_delta[:], per_delta[:], delta[:])
+        fma(dd[:], delta[:], delta[:])
+        fma(shift_1[:], delta[:], shift_d[:], shift_0[:])
+        fma(c2_0[:], s_tt[:], alpha_r[:])
+        fma(c3_0[:], s_tt[:], alpha_sigma)
+        fma(c3_1[:], dd[:], c3_dd[:], c3_0[:])
+        fma(shift[:], s_ta[:], half_rho_sigma[:], shift_1[:])
+        fma(coef_p[:], s_ta[:], by_delta[:, 2:3], c2_0[:])
+        fma(coef_a[:], s_ta[:], by_delta[:, 1:2], c3_1[:])
+        fma(shift_sq[:], shift[:], shift[:])
+
+        square = wide("square")
+        sum_ta, neg_sum_p, sum_a, result = (wide(n) for n in ("sum_ta", "neg_sum_p", "sum_a", "result"))
+        for cols in HALVES:
+            nc.scalar.activation(out=square[:, cols], in_=pc[:, cols], func=ACT.Square, scale=rho_r[:], bias=shift[:])
+        for cols in HALVES:
+            stt(sum_ta[:, cols], ta[:, cols], by_delta[:, 0:1], ALU.mult, base_sb[:, cols], ALU.add)
+        for cols in HALVES:
+            stt(neg_sum_p[:, cols], p[:, cols], coef_p[:], ALU.mult, sum_ta[:, cols], ALU.subtract)
+            stt(sum_a[:, cols], a[:, cols], coef_a[:], ALU.mult, square[:, cols], ALU.add)
+        for cols, queue in zip(HALVES, (nc.sync, nc.scalar)):
+            stt(result[:, cols], sum_a[:, cols], shift_sq[:], ALU.subtract, neg_sum_p[:, cols], ALU.subtract)
+            queue.dma_start(out=out[:, cols], in_=result[:, cols])

from contextlib import ExitStack

import concourse.mybir as mybir

D, E, T, I, Q = 512, 512, 2048, 512, 128
FLOPS = 2 * Q * I * (D + E)

F32 = mybir.dt.float32
BF16 = mybir.dt.bfloat16
I32 = mybir.dt.int32
U32 = mybir.dt.uint32
U16 = mybir.dt.uint16
U8 = mybir.dt.uint8
FP8X4 = mybir.dt.float8_e4m3fn_x4
ALU = mybir.AluOpType
ACT = mybir.ActivationFunctionType

P = 128
PACK = 4
BLOCKS = 16
LIST_ROWS = 16
RHO_SCALE = 2.0**8.5
KEYS_FIRST, VALS_FIRST = 0, 4
HALVES = (slice(0, I // 2), slice(I // 2, I))


def tile_attend_gpevenbyspread_kernel(tc, query, keys_words, keys_scales, th, gout, vals_words, vals_scales, base, offs, out):
    nc = tc.nc

    with ExitStack() as ctx:
        sb = ctx.enter_context(tc.tile_pool(name="sb", bufs=1))
        ps = ctx.enter_context(tc.psum_pool(name="ps", bufs=1))

        def col(name, width=1):
            return sb.tile([P, width], F32, name=name)

        def wide(name):
            return sb.tile([P, I], F32, name=name)

        def fma(dst, x, scale, bias=0.0):
            nc.scalar.activation(out=dst, in_=x, func=ACT.Identity, scale=scale, bias=bias)

        def stt(dst, x, scalar, op0, y, op1, total=None):
            nc.vector.scalar_tensor_tensor(out=dst, in0=x, scalar=scalar, in1=y, op0=op0, op1=op1, accum_out=total)

        offsets = sb.tile([P, I // LIST_ROWS], U16, name="offsets")
        k_word_pool = sb.tile([P, T], I32, name="k_word_pool")
        v_word_pool = sb.tile([P, T], I32, name="v_word_pool", tag="v_words")
        k_byte_pool = sb.tile([P, T], U8, name="k_byte_pool", tag="k_bytes", align_bytes=64)
        v_byte_pool = sb.tile([P, T], U8, name="v_byte_pool", tag="v_bytes")
        q_raw = sb.tile([P, PACK, Q], F32, name="q_raw")
        g_raw = sb.tile([P, PACK, Q], F32, name="g_raw")
        th_sb, base_sb = col("th_sb"), wide("base_sb")

        nc.vector.memset(k_byte_pool[:].bitcast(I32), 0)
        nc.vector.memset(v_byte_pool[:].bitcast(I32), 0)

        def load_scale_bytes(queues, pool, first, src):
            for j in range(4):
                queues[j].dma_start(out=pool[first + j : P : 32, :].bitcast(I32), in_=src[0, j:BLOCKS:4, :].bitcast(I32))

        def load_words(pool, src):
            nc.sync.dma_start(out=pool[:], in_=src[0].rearrange("p n t -> p (n t)").bitcast(I32))

        def load_rows(raw, src):
            nc.sync.dma_start(out=raw[:], in_=src.rearrange("(p j) w -> p j w", j=PACK))

        nc.sync.dma_start(offsets[:], offs)
        load_rows(q_raw, query)
        load_scale_bytes([nc.sync, nc.sync, nc.scalar, nc.scalar], k_byte_pool, KEYS_FIRST, keys_scales)
        load_words(k_word_pool, keys_words)
        load_scale_bytes([nc.sync] * 4, v_byte_pool, VALS_FIRST, vals_scales)
        load_rows(g_raw, gout)
        load_words(v_word_pool, vals_words)
        nc.sync.dma_start(out=th_sb[:], in_=th)
        nc.sync.dma_start(out=base_sb[:], in_=base)

        def quantize(raw, name, codes_tag):
            grouped = sb.tile([P, Q, PACK], BF16, name=name + "_bf16", align_bytes=64)
            codes = sb.tile([P, Q], U32, name=name + "_codes", tag=codes_tag, align_bytes=64)
            scales = sb.tile([P, Q], U8, name=name + "_scales", align_bytes=64)
            nc.scalar.copy(out=grouped[:], in_=raw[:].rearrange("p j w -> p w j"))
            nc.vector.quantize_mx(out=codes[:].bitcast(FP8X4), scales=scales[:], in_=grouped[:].rearrange("p w j -> p (w j)"))
            return codes, scales

        def gather_bytes(pool, name):
            picked = sb.tile([P, I], U8, name=name, align_bytes=64)
            nc.vector.tensor_copy(picked[:], pool[:].indirect(offsets[:]))
            return picked

        def gather_words(pool, name):
            picked = sb.tile([P, I], U32, name=name, align_bytes=64)
            for cols in HALVES:
                entries = offsets[:, cols.start // LIST_ROWS : cols.stop // LIST_ROWS]
                nc.vector.tensor_copy(picked[:, cols], pool[:].bitcast(U32).indirect(entries))
            return picked

        def multiply(acc, stationary, words, scale_bytes, first, cols):
            codes, scales = stationary
            nc.tensor.matmul_mx(
                out=acc, lhsT=codes[:].bitcast(FP8X4), lhsT_scale=scales[:],
                rhs=words[:, cols].bitcast(FP8X4), rhs_scale=scale_bytes[first:P, cols], start=True, stop=True,
            )

        k_bytes = gather_bytes(k_byte_pool, "k_bytes_picked")
        q_mx = quantize(q_raw, "q", "k_bytes")
        k_words = gather_words(k_word_pool, "k_words_picked")
        a = ps.tile([P, I], F32, name="a")
        for cols in HALVES:
            multiply(a[:, cols], q_mx, k_words, k_bytes, KEYS_FIRST, cols)
        v_bytes = gather_bytes(v_byte_pool, "v_bytes_picked")
        g_mx = quantize(g_raw, "g", "g_codes")

        neg_a, neg_max = sb.tile([P, I], F32, name="neg_a", tag="v_bytes"), col("neg_max")
        nc.vector.tensor_scalar(out=neg_a[:], in0=a[:], scalar1=-1.0, scalar2=None, op0=ALU.mult, op1=ALU.min, accum_out=neg_max[:])
        p, z = wide("p"), col("z")
        nc.scalar.activation(out=p[:], in_=neg_a[:], func=ACT.Exp, scale=-1.0, bias=neg_max[:], accum_out=z[:])

        v_words = gather_words(v_word_pool, "v_words_picked")
        c = ps.tile([P, I], F32, name="c")
        for cols in HALVES:
            multiply(c[:, cols], g_mx, v_words, v_bytes, VALS_FIRST, cols)
        c_again = ps.tile([P, I // 2], F32, name="c_again")
        multiply(c_again[:], g_mx, v_words, v_bytes, VALS_FIRST, HALVES[0])

        factors = sb.tile([P, 2], F32, name="factors", tag="v_words")
        r = factors[:, 1:2]
        nc.vector.reciprocal(out=r, in_=z[:])
        aw, s_aw = wide("aw"), col("s_aw")
        stt(aw[:], a[:], r, ALU.mult, p[:], ALU.mult, s_aw[:])

        a_sq, s_aa64, tau, pp, s_pp = wide("a_sq"), col("s_aa64"), col("tau"), wide("pp"), col("s_pp")
        nc.scalar.activation(out=a_sq[:], in_=neg_a[:], func=ACT.Square, scale=0.125, accum_out=s_aa64[:])
        th2 = col("th2")
        fma(th2[:], th_sb[:], 2.0)
        nc.scalar.activation(out=tau[:], in_=s_aa64[:], func=ACT.Tanh, scale=-2.0 * 64 / I, bias=th2[:])
        nc.scalar.activation(out=pp[:], in_=p[:], func=ACT.Square, accum_out=s_pp[:])

        sigma, rho, rr, s, rho4, one_nu, one_aw = (col(n) for n in ("sigma", "rho", "rr", "s", "rho4", "one_nu", "one_aw"))
        fma(sigma[:], tau[:], 1.0 / 128, 1.0 / 128)
        fma(rho[:], tau[:], -RHO_SCALE, RHO_SCALE)
        fma(rr[:], r, r)
        fma(s[:], tau[:], 0.5, 0.5)
        fma(rho4[:], tau[:], -RHO_SCALE / 4, RHO_SCALE / 4)
        fma(factors[:, 0:1], tau[:], 3.0 / 128, 1.0 / 128)
        fma(one_nu[:], tau[:], s_aa64[:], 1.0)
        fma(one_aw[:], s_aw[:], -1.0, 1.0)

        rho_sigma, neg2rr, rho_r, sigma_nu, kappa_in_c1 = (
            col(n) for n in ("rho_sigma", "neg2rr", "rho_r", "sigma_nu", "kappa_in_c1")
        )
        neg_pp = col("neg_pp", 2)
        fma(rho_sigma[:], sigma[:], rho[:])
        fma(neg2rr[:], rr[:], -2.0)
        fma(rho_r[:], r, rho[:])
        fma(neg_pp[:, 0:1], s_pp[:], -0.5)
        fma(neg_pp[:, 1:2], s_pp[:], -1.0)
        fma(sigma_nu[:], sigma[:], one_nu[:])
        fma(kappa_in_c1[:], s[:], s_aa64[:], one_aw[:])

        per_delta = col("per_delta", 3)
        alpha_sigma = per_delta[:, 0:1]
        half_rho_sigma, alpha_r, shift_pt, c3_dd, shift_d = (
            col(n) for n in ("half_rho_sigma", "alpha_r", "shift_pt", "c3_dd", "shift_d")
        )
        fma(alpha_sigma, rho_sigma[:], rho[:])
        fma(half_rho_sigma[:], rho_sigma[:], 0.5)
        fma(alpha_r[:], rho_r[:], rho[:])
        fma(shift_pt[:], neg2rr[:], rho4[:])
        fma(per_delta[:, 1:3], factors[:], alpha_sigma)
        fma(c3_dd[:], sigma_nu[:], alpha_sigma)
        fma(shift_d[:], kappa_in_c1[:], half_rho_sigma[:])

        wc, m = wide("wc"), col("m")
        c_scaled, delta, mean_0, mean_1 = wide("c_scaled"), col("delta"), col("mean_0"), col("mean_1")
        nc.scalar.activation(out=c_scaled[:, HALVES[0]], in_=c_again[:], func=ACT.Identity, scale=-1.0 / I, accum_out=mean_0[:])
        ppc, s_ppc = wide("ppc"), col("s_ppc")
        ta, s_ta = wide("ta"), col("s_ta")
        pc = wide("pc")
        stt(wc[:], c[:], r, ALU.mult, p[:], ALU.mult, m[:])
        stt(ppc[:], c[:], 1.0, ALU.mult, pp[:], ALU.mult, s_ppc[:])
        nc.vector.tensor_scalar(out=c_scaled[:, HALVES[1]], in0=c[:, HALVES[1]], scalar1=-1.0 / I, scalar2=m[:], op0=ALU.mult, op1=ALU.add, accum_out=mean_1[:])
        stt(ta[:], c[:], m[:], ALU.subtract, aw[:], ALU.mult, s_ta[:])
        stt(pc[:], c[:], m[:], ALU.subtract, p[:], ALU.mult)

        wc_sq, s_wcwc = wide("wc_sq"), col("s_wcwc")
        nc.scalar.activation(out=wc_sq[:], in_=wc[:], func=ACT.Square, accum_out=s_wcwc[:])
        neg2mrr, dd, shift_0, shift_1, c3_0, c3_1, c2_0 = (
            col(n) for n in ("neg2mrr", "dd", "shift_0", "shift_1", "c3_0", "c3_1", "c2_0")
        )
        shift, shift_sq, coef_a, coef_p = (col(n) for n in ("shift", "shift_sq", "coef_a", "coef_p"))
        s_tt = col("s_tt")
        centred = col("centred", 2)
        by_delta = col("by_delta", 3)
        fma(neg2mrr[:], m[:], neg2rr[:])
        fma(centred[:], neg_pp[:], m[:], s_ppc[:])
        fma(delta[:], mean_1[:], 1.0, mean_0[:])
        fma(s_tt[:], centred[:, 0:1], neg2mrr[:], s_wcwc[:])
        fma(shift_0[:], centred[:, 1:2], shift_pt[:])
        fma(by_delta[:], per_delta[:], delta[:])
        fma(dd[:], delta[:], delta[:])
        fma(shift_1[:], delta[:], shift_d[:], shift_0[:])
        fma(c2_0[:], s_tt[:], alpha_r[:])
        fma(c3_0[:], s_tt[:], alpha_sigma)
        fma(c3_1[:], dd[:], c3_dd[:], c3_0[:])
        fma(shift[:], s_ta[:], half_rho_sigma[:], shift_1[:])
        fma(coef_p[:], s_ta[:], by_delta[:, 2:3], c2_0[:])
        fma(coef_a[:], s_ta[:], by_delta[:, 1:2], c3_1[:])
        fma(shift_sq[:], shift[:], shift[:])

        square = wide("square")
        sum_ta, neg_sum_p, sum_a, result = (wide(n) for n in ("sum_ta", "neg_sum_p", "sum_a", "result"))
        for cols in HALVES:
            nc.scalar.activation(out=square[:, cols], in_=pc[:, cols], func=ACT.Square, scale=rho_r[:], bias=shift[:])
        for cols in HALVES:
            stt(sum_ta[:, cols], ta[:, cols], by_delta[:, 0:1], ALU.mult, base_sb[:, cols], ALU.add)
        for cols in HALVES:
            stt(neg_sum_p[:, cols], p[:, cols], coef_p[:], ALU.mult, sum_ta[:, cols], ALU.subtract)
            stt(sum_a[:, cols], a[:, cols], coef_a[:], ALU.mult, square[:, cols], ALU.add)
        for cols, queue in zip(HALVES, (nc.sync, nc.scalar)):
            stt(result[:, cols], sum_a[:, cols], shift_sq[:], ALU.subtract, neg_sum_p[:, cols], ALU.subtract)
            queue.dma_start(out=out[:, cols], in_=result[:, cols])
